import numpy as np
CORES = [96,97,98,99,224,225,226,227,352,353,354,355,480,481,482,483]
N = 16
GROUPS = [[0,1,2,3],[4,5,6,7],[8,9,10,11],[12,13,14,15]]
def setup_inputs(rng):
    return {"x": rng.standard_normal((N, 128, 256), dtype=np.float32)}
def reference(x):
    y = np.empty((N, 128, 64), x.dtype)
    for g in GROUPS:
        s = x[g].sum(axis=0, dtype=np.float64).astype(x[g].dtype)
        n = len(g); b = x.shape[2] // n
        for i, r in enumerate(g):
            y[r] = s[:, i * b:(i + 1) * b]
    return {"y": y}

@@ -1,0 +1,43 @@
+from concourse.bass import DstId, RemoteDMATransfer
+from concourse.mybir import AluOpType
+
+SCRATCH = {
+    "xs": ("sbuf", [128, 256], "float32"),
+    "land": ("sbuf", [128, 256], "float32"),
+}
+SEMAPHORES = ["loaded", "own", "left", "arrived", "acc", "stored"]
+
+
+def rank_program(g, core, T, topo):
+    rank = T.rank_of(core)
+    if rank is None:
+        return
+    group = [m for m in T.tables["GROUPS"] if rank in m][0]
+    n = len(group)
+    i = group.index(rank)
+    b = T.x.shape[1] // n
+
+    def blk(k):
+        return slice(k * b, (k + 1) * b)
+
+    g.sync.dma_start(T.land[:, blk(i)], T.x[:, blk(i)]).then_inc(T.sem.own, 16)
+    g.dma_start(T.xs[:], T.x[:]).then_inc(T.sem.loaded, 16)
+    g.wait_ge(T.sem.loaded, 16)
+
+    transfers = []
+    for t, j in enumerate([k for k in range(n) if k != i]):
+        rid, pid = topo.addr(T.cores[group[j]], core)
+        transfers.append(RemoteDMATransfer(
+            dst_ids=[DstId(rid=rid, pnc=pid)], dma_engine_mask=0xF << (4 * t), remote_sem=T.sem.arrived,
+            src=T.xs[:, blk(j)], dst=T.land[:, blk(i)]))
+    g.remote_dma_fused(transfers, local_sem=T.sem.left)
+
+    g.wait_ge(T.sem.own, 16)
+    g.wait_ge(T.sem.arrived, 4 * (n - 1))
+    g.dma_start(T.land[:, 0:2 * b], T.land[:, 2 * b:4 * b], accum_op=AluOpType.add).then_inc(T.sem.acc, 16)
+    g.wait_ge(T.sem.acc, 16)
+    g.dma_start(T.land[:, 0:b], T.land[:, b:2 * b], accum_op=AluOpType.add).then_inc(T.sem.acc, 16)
+    g.wait_ge(T.sem.acc, 32)
+    g.dma_start(T.y[:], T.land[:, 0:b]).then_inc(T.sem.stored, 16)
+    g.wait_ge(T.sem.stored, 16)
+    g.wait_ge(T.sem.left, 4 * (n - 1))

@@ -3,9 +3,10 @@ from concourse.mybir import AluOpType
 
 SCRATCH = {
     "xs": ("sbuf", [128, 256], "float32"),
-    "land": ("sbuf", [128, 256], "float32"),
+    "land": ("sbuf", [128, 128], "float32"),
+    "part": ("sbuf", [128, 64], "float32"),
 }
-SEMAPHORES = ["loaded", "own", "left", "arrived", "acc", "stored"]
+SEMAPHORES = ["loaded", "own", "arrived", "folded", "left", "done"]
 
 
 def rank_program(g, core, T, topo):
@@ -20,24 +21,35 @@ def rank_program(g, core, T, topo):
     def blk(k):
         return slice(k * b, (k + 1) * b)
 
-    g.sync.dma_start(T.land[:, blk(i)], T.x[:, blk(i)]).then_inc(T.sem.own, 16)
-    g.dma_start(T.xs[:], T.x[:]).then_inc(T.sem.loaded, 16)
-    g.wait_ge(T.sem.loaded, 16)
+    def dst_id(member):
+        rid, pid = topo.addr(T.cores[group[member]], core)
+        return DstId(rid=rid, pnc=pid)
 
-    transfers = []
-    for t, j in enumerate([k for k in range(n) if k != i]):
-        rid, pid = topo.addr(T.cores[group[j]], core)
-        transfers.append(RemoteDMATransfer(
-            dst_ids=[DstId(rid=rid, pnc=pid)], dma_engine_mask=0xF << (4 * t), remote_sem=T.sem.arrived,
-            src=T.xs[:, blk(j)], dst=T.land[:, blk(i)]))
-    g.remote_dma_fused(transfers, local_sem=T.sem.left)
+    def copiers(j):
+        return [m for m in range(n) if m != j and m != (j + 1) % n]
+
+    g.sync.dma_start(T.xs[:], T.x[:]).then_inc(T.sem.loaded, 16)
+    g.scalar.dma_start(T.y[:], T.x[:, blk(i)]).then_inc(T.sem.own, 16)
+
+    fold_blk = (i - 1) % n
+    sends = [j for j in range(n) if j != i and j != fold_blk]
+    eng = 16 // len(sends)
+    g.wait_ge(T.sem.loaded, 16)
+    g.remote_dma_fused([
+        RemoteDMATransfer(
+            dst_ids=[dst_id((j + 1) % n)], dma_engine_mask=((1 << eng) - 1) << (eng * t), remote_sem=T.sem.arrived,
+            src=T.xs[:, blk(j)], dst=T.land[:, blk(copiers(j).index(i))])
+        for t, j in enumerate(sends)], local_sem=T.sem.left)
+
+    g.wait_ge(T.sem.arrived, eng * len(sends))
+    g.remote_dma_fused([
+        RemoteDMATransfer(
+            dst_ids=[dst_id(fold_blk)], dma_engine_mask=0xFFFF, remote_sem=T.sem.folded, alu_op=1,
+            srcs=[T.xs[:, blk(fold_blk)]] + [T.land[:, blk(s)] for s in range(len(sends))], dsts=[T.part[:]])],
+        local_sem=T.sem.left)
 
     g.wait_ge(T.sem.own, 16)
-    g.wait_ge(T.sem.arrived, 4 * (n - 1))
-    g.dma_start(T.land[:, 0:2 * b], T.land[:, 2 * b:4 * b], accum_op=AluOpType.add).then_inc(T.sem.acc, 16)
-    g.wait_ge(T.sem.acc, 16)
-    g.dma_start(T.land[:, 0:b], T.land[:, b:2 * b], accum_op=AluOpType.add).then_inc(T.sem.acc, 16)
-    g.wait_ge(T.sem.acc, 32)
-    g.dma_start(T.y[:], T.land[:, 0:b]).then_inc(T.sem.stored, 16)
-    g.wait_ge(T.sem.stored, 16)
-    g.wait_ge(T.sem.left, 4 * (n - 1))
+    g.wait_ge(T.sem.folded, 16)
+    g.dma_start(T.y[:], T.part[:], accum_op=AluOpType.add).then_inc(T.sem.done, 16)
+    g.wait_ge(T.sem.done, 16)
+    g.wait_ge(T.sem.left, eng * len(sends) + 16)

from concourse.bass import DstId, RemoteDMATransfer
from concourse.mybir import AluOpType

SCRATCH = {
    "xs": ("sbuf", [128, 256], "float32"),
    "land": ("sbuf", [128, 128], "float32"),
    "part": ("sbuf", [128, 64], "float32"),
}
SEMAPHORES = ["loaded", "own", "arrived", "folded", "left", "done"]


def rank_program(g, core, T, topo):
    rank = T.rank_of(core)
    if rank is None:
        return
    group = [m for m in T.tables["GROUPS"] if rank in m][0]
    n = len(group)
    i = group.index(rank)
    b = T.x.shape[1] // n

    def blk(k):
        return slice(k * b, (k + 1) * b)

    def dst_id(member):
        rid, pid = topo.addr(T.cores[group[member]], core)
        return DstId(rid=rid, pnc=pid)

    def copiers(j):
        return [m for m in range(n) if m != j and m != (j + 1) % n]

    g.sync.dma_start(T.xs[:], T.x[:]).then_inc(T.sem.loaded, 16)
    g.scalar.dma_start(T.y[:], T.x[:, blk(i)]).then_inc(T.sem.own, 16)

    fold_blk = (i - 1) % n
    sends = [j for j in range(n) if j != i and j != fold_blk]
    eng = 16 // len(sends)
    g.wait_ge(T.sem.loaded, 16)
    g.remote_dma_fused([
        RemoteDMATransfer(
            dst_ids=[dst_id((j + 1) % n)], dma_engine_mask=((1 << eng) - 1) << (eng * t), remote_sem=T.sem.arrived,
            src=T.xs[:, blk(j)], dst=T.land[:, blk(copiers(j).index(i))])
        for t, j in enumerate(sends)], local_sem=T.sem.left)

    g.wait_ge(T.sem.arrived, eng * len(sends))
    g.remote_dma_fused([
        RemoteDMATransfer(
            dst_ids=[dst_id(fold_blk)], dma_engine_mask=0xFFFF, remote_sem=T.sem.folded, alu_op=1,
            srcs=[T.xs[:, blk(fold_blk)]] + [T.land[:, blk(s)] for s in range(len(sends))], dsts=[T.part[:]])],
        local_sem=T.sem.left)

    g.wait_ge(T.sem.own, 16)
    g.wait_ge(T.sem.folded, 16)
    g.dma_start(T.y[:], T.part[:], accum_op=AluOpType.add).then_inc(T.sem.done, 16)
    g.wait_ge(T.sem.done, 16)
    g.wait_ge(T.sem.left, eng * len(sends) + 16)
